import numpy as np
import ml_dtypes


def mxq(x, axis, fmt="e4m3"):
    dtype, down = {"e4m3": (ml_dtypes.float8_e4m3fn, 7), "e5m2": (ml_dtypes.float8_e5m2, 14)}[fmt]
    v = np.moveaxis(np.asarray(x, np.float32).astype(ml_dtypes.bfloat16).astype(np.float64), axis, -1)
    blocks = v.reshape(v.shape[:-1] + (-1, 32))
    amax = np.abs(blocks).max(-1, keepdims=True)
    byte = np.maximum(np.where(amax > 0, np.frexp(amax)[1] - 1 + 127, 0) - down, 1)
    scale = np.exp2(byte - 127.0)
    codes = (blocks / scale).astype(np.float32).astype(dtype).astype(np.float64)
    return np.moveaxis((codes * scale).reshape(v.shape), -1, axis)


WIDE = False


def mx_kscale(k):
    if not WIDE:
        return np.ones(k)
    levels = np.array([10, -10, 5, -5, 0])
    if k % 512:
        return np.exp2(np.random.permutation(np.resize(levels, k // 32))).repeat(32)
    a = np.empty((k // 512, 16))
    for p in range(k // 512):
        a[p, :8] = np.random.permutation(np.resize(levels, 8))
        for g in range(8):
            far = levels[np.abs(levels - a[p, g]) >= 10]
            a[p, g + 8] = far[np.random.randint(len(far))]
    return np.exp2(a.ravel()).repeat(32)


BF16 = ml_dtypes.bfloat16


def bf(x):
    return np.asarray(x, np.float32).astype(BF16)


def f64(x):
    return np.asarray(x).astype(np.float64)


E2M1 = np.array([0.0, 0.5, 1.0, 1.5, 2.0, 3.0, 4.0, 6.0, -0.0, -0.5, -1.0, -1.5, -2.0, -3.0, -4.0, -6.0])


def pack_weight(w, fmt):
    k, n = w.shape
    w = f64(bf(w)).reshape(k // 32, 32, n)
    amax = np.abs(w).max(1)
    if fmt == "e4m3":
        byte = np.frexp(amax)[1] - 1 + 127 - 7
    else:
        mant, ex = np.frexp(amax / 6.0)
        byte = np.where(mant > 0.5, ex, ex - 1) + 127
    byte = np.clip(np.where(amax > 0, byte, 1), 1, 254)
    scaled = (w * np.exp2(127.0 - byte)[:, None, :]).reshape(k, n).astype(np.float32)
    by_word = np.ascontiguousarray(scaled.reshape(k // 512, 128, 4, n).transpose(0, 1, 3, 2))
    if fmt == "e4m3":
        words = by_word.astype(ml_dtypes.float8_e4m3fn).view(np.uint8)
    else:
        c = by_word.astype(ml_dtypes.float4_e2m1fn).view(np.uint8) & 0xF
        words = c[..., 0::2] | (c[..., 1::2] << 4)
    return np.ascontiguousarray(words), np.ascontiguousarray(byte.astype(np.uint8).reshape(k // 512, 16, n))


def unpack_weight(words, scales, fmt):
    g, p, n, _ = words.shape
    if fmt == "e4m3":
        vals = np.ascontiguousarray(words).view(ml_dtypes.float8_e4m3fn).astype(np.float64)
    else:
        nib = np.empty((g, p, n, 4), np.uint8)
        nib[..., 0::2] = words & 0xF
        nib[..., 1::2] = words >> 4
        vals = E2M1[nib]
    vals = vals * np.repeat(np.exp2(scales.astype(np.float64) - 127.0), 8, axis=1)[..., None]
    return vals.transpose(0, 1, 3, 2).reshape(g * 512, n)
def pack4(w):
    words, scales = pack_weight(w, "e2m1")
    return words.reshape(words.shape[0], 128, -1), scales


def unpack4(words, scales):
    return unpack_weight(words.reshape(words.shape[0], 128, -1, 2), scales, "e2m1")


def planes(Y):
    n, m = Y.shape
    b = f64(bf(Y)).reshape(n // 32, 32, m)
    amax = np.abs(b).max(1)
    byte = np.clip(np.where(amax > 0, np.frexp(amax)[1] - 1 + 127 - 7, 1), 1, 254)
    codes = (b * np.exp2(127.0 - byte)[:, None, :]).reshape(n, m).astype(np.float32).astype(ml_dtypes.float8_e4m3fn).view(np.uint8)
    words = codes.reshape(n // 512, 128, 4, m).transpose(0, 1, 3, 2)
    return np.ascontiguousarray(words), np.ascontiguousarray(byte.astype(np.uint8).reshape(n // 512, 16, m))


T, KL, KH, N, SEG = 2048, 512, 2048, 512, 64
NYQUIST, HALF = 8000.0, 16.0

def mel(hz):
    return 1127.0 * np.log(1.0 + hz / 700.0)

def setup_inputs():
    K = KL + KH
    re, im = np.random.randn(T, K), np.random.randn(T, K)
    loud = np.exp(2.0 + 0.6 * np.random.randn(T, 1))
    envelope = np.repeat(np.exp(0.5 * np.random.randn(T, K // SEG)), SEG, axis=1)
    tilt = 1.0 / (1.0 + 2.0 * np.arange(K) / K)
    power = 0.5 * (re ** 2 + im ** 2) * loud * envelope * tilt
    top = mel(NYQUIST)
    hz = (np.arange(K) + 0.5) / K * NYQUIST
    centre = (np.arange(N) + 0.5) / N * top
    tri = np.maximum(0.0, 1.0 - np.abs(mel(hz)[:, None] - centre[None, :]) / (HALF * top / N))
    bank = tri / tri.sum(axis=0) * np.exp(0.3 * np.random.randn(K, N)) + 0.3 / K * (0.5 + np.random.rand(K, N))
    sl, sh = mx_kscale(KL), mx_kscale(KH)
    words, scales = pack4(bank[KL:] / sh[:, None])
    return {"power_low": bf(power[:, :KL] * sl), "power_high": bf(power[:, KL:] * sh),
            "bank_low": bf(bank[:KL] / sl[:, None]), "bank_high_words": words, "bank_high_scales": scales,
            "least_energy": bf(np.exp(0.9 + 0.2 * np.random.randn(N))), "gain": bf(np.exp(0.8 * np.random.randn(N)))}

def reference(power_low, power_high, bank_low, bank_high_words, bank_high_scales, least_energy, gain):
    A = mxq(f64(power_low), 1, "e4m3")
    B = mxq(f64(bank_low), 0, "e4m3")
    low = A @ B
    C = mxq(f64(power_high), 1, "e4m3")
    D = unpack4(bank_high_words, bank_high_scales)
    high = C @ D
    y = np.log(np.maximum(low + high, f64(least_energy))) * f64(gain)
    Y = y.T
    words, scales = planes(Y)
    return y, words, scales

@@ -1,0 +1,303 @@
+from contextlib import ExitStack
+
+import concourse.mybir as mybir
+from concourse.masks import make_identity
+
+T, KL, KH, N = 2048, 512, 2048, 512
+FLOPS = 2 * T * (KL + KH) * N
+
+F32 = mybir.dt.float32
+BF16 = mybir.dt.bfloat16
+I32 = mybir.dt.int32
+U32 = mybir.dt.uint32
+U8 = mybir.dt.uint8
+FP8X4 = mybir.dt.float8_e4m3fn_x4
+FP4X4 = mybir.dt.float4_e2m1fn_x4
+ALU = mybir.AluOpType
+ACT = mybir.ActivationFunctionType
+
+P = 128
+TILES = T // P
+HIGH = KH // 512
+PASSES = HIGH + 1
+LOW = HIGH
+WORDS = 256
+
+V_SORT = (0, 1)
+S_SORT = (2, 3)
+FIRST_SORTED = 2
+Y_LAG = 4
+LOW_V = 352
+RING = 4
+
+
+def tile_split_band_log_mel_g5_kernel(
+    tc, power_low, power_high, bank_low, bank_high_words, bank_high_scales, least_energy, gain,
+    out_0, out_1, out_2,
+):
+    nc = tc.nc
+    with ExitStack() as ctx:
+        keep = ctx.enter_context(tc.tile_pool(name="keep", bufs=1))
+        psum = ctx.enter_context(tc.psum_pool(name="psum", bufs=1))
+
+        def ring(pool, label, count, shape, dtype):
+            return [pool.tile(shape, dtype, name=f"{label}{i}", align_bytes=64) for i in range(count)]
+
+        power = ring(keep, "power", TILES, [P, PASSES * 512], BF16)
+        sorted_words = ring(keep, "sorted", RING, [P, PASSES, 2, P], F32)
+        staged = ring(keep, "staged", RING, [P, (PASSES + 1) * 512], BF16)
+        codes = ring(keep, "codes", RING, [P, PASSES * P], U32)
+        scales = ring(keep, "scales", RING, [P, PASSES * P], U8)
+        clamped = ring(keep, "clamped", 2, [P, N], F32)
+        logs = ring(keep, "logs", RING, [P, N], F32)
+        y = ring(keep, "y", TILES, [P, N], F32)
+        y_bf = ring(keep, "y_bf", RING, [P, 2, P, 2], BF16)
+        y_codes = keep.tile([P, T], U32, align_bytes=64)
+        y_scales = keep.tile([P, T], U8, align_bytes=64)
+        high_words = keep.tile([P, HIGH, 2 * N], U8, align_bytes=64)
+        high_scales = keep.tile([P, HIGH, N], U8, align_bytes=64)
+        low_raw = keep.tile([P, 4, N], BF16, align_bytes=64)
+        low_grouped = keep.tile([P, N, 4], BF16, align_bytes=64)
+        low_codes = keep.tile([P, N], U32, align_bytes=64)
+        low_scales = keep.tile([P, N], U8, align_bytes=64)
+        least_col = keep.tile([P, 4], BF16, align_bytes=64)
+        gain_col = keep.tile([P, 4], BF16, align_bytes=64)
+        band_rows = keep.tile([P, 2, N], BF16, align_bytes=64)
+        ident = keep.tile([P, P], F32, align_bytes=64)
+        warm = keep.tile([P, 2], F32, align_bytes=64)
+        turn = [psum.tile([P, 4, P], F32, name=f"turn{i}") for i in range(6)]
+        energy = [psum.tile([P, N], F32, name=f"energy{i}") for i in range(2)]
+
+        ctx.enter_context(tc.manual_schedule())
+
+        def load_power(i, pieces):
+            rows = slice(i * P, (i + 1) * P)
+            step = KH // pieces
+            for c in range(0, KH, step):
+                nc.sync.dma_start(out=power[i][:, c : c + step], in_=power_high[rows, c : c + step])
+            nc.sync.dma_start(out=power[i][:, KH:], in_=power_low[rows, :])
+
+        def sorted_by(i, g):
+            if i < FIRST_SORTED or i >= TILES:
+                return None
+            return "v" if g in V_SORT else "s" if g in S_SORT else None
+
+        def sort(i, who):
+            gs = [g for g in range(PASSES) if sorted_by(i, g) == who]
+            if not gs:
+                return
+            lo, hi = gs[0], gs[-1] + 1
+            src = power[i][:].bitcast(F32)[:, lo * WORDS : hi * WORDS].rearrange("m (g p u) -> m g u p", u=2, p=P)
+            dst = sorted_words[i % RING][:, lo:hi, :, :]
+            if who == "v":
+                nc.vector.tensor_copy(out=dst, in_=src)
+            else:
+                nc.scalar.copy(out=dst, in_=src)
+
+        def bank_of(s, slot):
+            return turn[3 * (s % 2) + slot // 2]
+
+        def transposes(s):
+            if s < TILES:
+                words = power[s][:].bitcast(F32)
+                for g in range(PASSES):
+                    for u in range(2):
+                        if sorted_by(s, g):
+                            src = sorted_words[s % RING][:, g, u, :]
+                        else:
+                            src = words[:, g * WORDS + u : (g + 1) * WORDS : 2]
+                        nc.tensor.transpose(bank_of(s, g)[:, 2 * (g % 2) + u, :], src, ident[:])
+            j = s - Y_LAG
+            if 0 <= j < TILES:
+                pairs = y_bf[j % RING][:].rearrange("m u p e -> m (u p e)").bitcast(F32)
+                for u in range(2):
+                    nc.tensor.transpose(bank_of(s, PASSES)[:, 2 + u, :], pairs[:, u * P : (u + 1) * P], ident[:])
+
+        def copy_out(s, b, copy=nc.scalar.copy):
+            lo, hi = 2 * b, 2 * b + 2
+            if s >= TILES:
+                lo = max(lo, PASSES)
+            if not 0 <= s - Y_LAG < TILES:
+                hi = min(hi, PASSES)
+            if lo >= hi:
+                return
+            dst = staged[s % RING][:].bitcast(F32)[:, lo * WORDS : hi * WORDS].rearrange("p (g m u) -> p g m u", u=2, m=P)
+            src = bank_of(s, lo)[:, 2 * (lo % 2) : 2 * (lo % 2) + 2 * (hi - lo), :].rearrange("p (g u) m -> p g m u", u=2)
+            copy(out=dst, in_=src)
+
+        def quantize_power(s, lo, hi):
+            if 0 <= s < TILES:
+                nc.vector.quantize_mx(
+                    out=codes[s % RING][:, lo * P : hi * P].bitcast(FP8X4),
+                    scales=scales[s % RING][:, lo * P : hi * P],
+                    in_=staged[s % RING][:, lo * 512 : hi * 512],
+                )
+
+        def quantize_y(j):
+            if 0 <= j < TILES:
+                cols = slice(j * P, (j + 1) * P)
+                nc.vector.quantize_mx(
+                    out=y_codes[:, cols].bitcast(FP8X4),
+                    scales=y_scales[:, cols],
+                    in_=staged[(j + Y_LAG) % RING][:, PASSES * 512 :],
+                )
+
+        def matmuls(i):
+            if not 0 <= i < TILES:
+                return
+            for g in range(PASSES):
+                cols = slice(g * P, (g + 1) * P)
+                if g == LOW:
+                    rhs, rhs_scale = low_codes[:].bitcast(FP8X4), low_scales[:]
+                else:
+                    rhs, rhs_scale = high_words[:, g, :].bitcast(FP4X4), high_scales[:, g, :]
+                nc.tensor.matmul_mx(
+                    out=energy[i % 2][:], lhsT=codes[i % RING][:, cols].bitcast(FP8X4), lhsT_scale=scales[i % RING][:, cols],
+                    rhs=rhs, rhs_scale=rhs_scale, start=(g == 0), stop=(g == PASSES - 1),
+                )
+
+        def clamp(j):
+            if 0 <= j < TILES:
+                nc.vector.tensor_tensor(out=clamped[j % 2][:], in0=energy[j % 2][:], in1=band_rows[:, 0, :], op=ALU.max)
+
+        def log(j):
+            if 0 <= j < TILES:
+                nc.scalar.activation(out=logs[j % RING][:], in_=clamped[j % 2][:], func=ACT.Ln)
+
+        def scale_and_store(j):
+            if 0 <= j < TILES:
+                nc.vector.tensor_tensor(out=y[j][:], in0=logs[j % RING][:], in1=band_rows[:, 1, :], op=ALU.mult)
+                nc.sync.dma_start(out=out_0[j * P : (j + 1) * P, :], in_=y[j][:])
+
+        def round_y(j, copy=nc.vector.tensor_copy):
+            if 0 <= j < TILES:
+                copy(out=y_bf[j % RING][:], in_=y[j][:].rearrange("m (p u e) -> m u p e", u=2, e=2))
+
+        out_words = out_1[0].rearrange("p m t -> p (m t)").bitcast(I32)
+        out_scales = out_2[0].bitcast(I32)
+
+        def store_planes(lo, hi):
+            nc.sync.dma_start(out=out_words[:, lo * P : hi * P], in_=y_codes[:, lo * P : hi * P].bitcast(I32))
+
+        def store_scales(lo, hi):
+            for q in range(4):
+                queue = nc.scalar if (hi == TILES and q % 2) else nc.sync
+                queue.dma_start(
+                    out=out_scales[4 * q : 4 * q + 4, lo * P // 4 : hi * P // 4],
+                    in_=y_scales[32 * q : 32 * q + 4, lo * P : hi * P].bitcast(I32),
+                )
+
+        nc.vector.memset(high_scales[:].rearrange("p g n -> p (g n)").bitcast(I32), 0)
+        nc.vector.memset(warm[:, 0:1], 1.0)
+        nc.scalar.activation(out=warm[:, 1:2], in_=warm[:, 0:1], func=ACT.Ln)
+        make_identity(nc, ident[:])
+        load_power(0, 2)
+        nc.sync.dma_start(out=least_col[:], in_=least_energy.rearrange("(p t) -> p t", t=4))
+        nc.sync.dma_start(out=gain_col[:], in_=gain.rearrange("(p t) -> p t", t=4))
+        nc.sync.dma_start(out=low_raw[:], in_=bank_low.rearrange("(p t) n -> p t n", t=4))
+        for q in range(4):
+            nc.sync.dma_start(
+                out=high_scales[32 * q : 32 * q + 4, :, :].bitcast(I32),
+                in_=bank_high_scales[:, 4 * q : 4 * q + 4, :].bitcast(I32).rearrange("g r n -> r g n"),
+            )
+        nc.sync.dma_start(out=high_words[:].bitcast(I32), in_=bank_high_words.bitcast(I32).rearrange("g p w -> p g w"))
+        for i in range(1, TILES):
+            load_power(i, 1)
+
+        band_bank = energy[1][:].rearrange("p (v m) -> p v m", m=P)
+
+        def spread_band_vectors():
+            for v, col in enumerate((least_col, gain_col)):
+                for u in range(2):
+                    src = col[:].bitcast(F32)[:, u : u + 1].to_broadcast([P, P])
+                    nc.tensor.transpose(band_bank[:, 2 * v + u, :], src, ident[:])
+
+        def copy_band_vectors():
+            nc.scalar.copy(
+                out=band_rows[:].rearrange("p v n -> p (v n)").bitcast(F32).rearrange("p (v m u) -> p v m u", u=2, m=P),
+                in_=band_bank.rearrange("p (v u) m -> p v m u", u=2),
+            )
+
+        def group_bank_low(copy, cols):
+            copy(
+                out=low_grouped[:, cols, :].rearrange("p (c i) t -> p c t i", i=4),
+                in_=low_raw[:, :, cols].rearrange("p t (c i) -> p c t i", i=4),
+            )
+
+        def quantize_bank_low():
+            nc.vector.quantize_mx(
+                out=low_codes[:].bitcast(FP8X4), scales=low_scales[:], in_=low_grouped[:].rearrange("p n t -> p (n t)")
+            )
+
+        def planes(j):
+            quantize_y(j)
+            done = j + 1
+            if done in (4, 8, 12, 15, 16):
+                store_planes({4: 0, 8: 4, 12: 8, 15: 12, 16: 15}[done], done)
+            if done in (12, 16):
+                store_scales(done - 12 if done == 12 else 12, done)
+
+        vector_copy = nc.vector.tensor_copy
+
+        transposes(0)
+        spread_band_vectors()
+        copy_out(0, 0)
+        copy_out(0, 1, vector_copy)
+        group_bank_low(nc.scalar.copy, slice(LOW_V, N))
+        group_bank_low(vector_copy, slice(0, LOW_V))
+        copy_out(0, 2)
+        quantize_power(0, 0, HIGH)
+        quantize_bank_low()
+        quantize_power(0, LOW, PASSES)
+        copy_band_vectors()
+        matmuls(0)
+
+        transposes(1)
+        clamp(0)
+        copy_out(1, 0)
+        sort(2, "v")
+        sort(2, "s")
+        copy_out(1, 1, vector_copy)
+        copy_out(1, 2)
+        log(0)
+        quantize_power(1, 0, HIGH)
+        quantize_power(1, LOW, PASSES)
+        sort(3, "s")
+        sort(3, "v")
+
+        for s in range(2, TILES):
+            transposes(s)
+            for b in range(3):
+                copy_out(s, b)
+            matmuls(s - 1)
+            sort(s + 2, "v")
+            quantize_power(s, 0, HIGH)
+            quantize_power(s, LOW, PASSES)
+            if s > 2:
+                log(s - 2)
+            clamp(s - 1)
+            scale_and_store(s - 2)
+            sort(s + 2, "s")
+            planes(s - Y_LAG)
+            round_y(s - 2)
+
+        matmuls(15)
+        transposes(16)
+        log(14)
+        copy_out(16, 2)
+        transposes(17)
+        clamp(15)
+        scale_and_store(14)
+        log(15)
+        copy_out(17, 2)
+        planes(12)
+        round_y(14)
+        scale_and_store(15)
+        transposes(18)
+        planes(13)
+        round_y(15)
+        copy_out(18, 2)
+        transposes(19)
+        copy_out(19, 2)
+        planes(14)
+        planes(15)

@@ -18,17 +18,16 @@ ACT = mybir.ActivationFunctionType
 
 P = 128
 TILES = T // P
+PAIRS = TILES // 2
 HIGH = KH // 512
-PASSES = HIGH + 1
-LOW = HIGH
 WORDS = 256
 
 V_SORT = (0, 1)
-S_SORT = (2, 3)
+S_SORT = (2,)
 FIRST_SORTED = 2
-Y_LAG = 4
 LOW_V = 352
 RING = 4
+LONG_RUNS = 0
 
 
 def tile_split_band_log_mel_g5_kernel(
@@ -40,26 +39,31 @@ def tile_split_band_log_mel_g5_kernel(
         keep = ctx.enter_context(tc.tile_pool(name="keep", bufs=1))
         psum = ctx.enter_context(tc.psum_pool(name="psum", bufs=1))
 
-        def ring(pool, label, count, shape, dtype):
-            return [pool.tile(shape, dtype, name=f"{label}{i}", align_bytes=64) for i in range(count)]
+        def ring(label, count, shape, dtype):
+            return [keep.tile(shape, dtype, name=f"{label}{i}", align_bytes=64) for i in range(count)]
 
-        power = ring(keep, "power", TILES, [P, PASSES * 512], BF16)
-        sorted_words = ring(keep, "sorted", RING, [P, PASSES, 2, P], F32)
-        staged = ring(keep, "staged", RING, [P, (PASSES + 1) * 512], BF16)
-        codes = ring(keep, "codes", RING, [P, PASSES * P], U32)
-        scales = ring(keep, "scales", RING, [P, PASSES * P], U8)
-        clamped = ring(keep, "clamped", 2, [P, N], F32)
-        logs = ring(keep, "logs", RING, [P, N], F32)
-        y = ring(keep, "y", TILES, [P, N], F32)
-        y_bf = ring(keep, "y_bf", RING, [P, 2, P, 2], BF16)
+        high = ring("high", PAIRS, [P, 2, KH], BF16)
+        low = ring("low", PAIRS, [P, 2, KL], BF16)
+        sorted_words = ring("sorted", 3, [P, 2, HIGH, 2, P], F32)
+        staged_high = ring("staged_high", RING, [P, KH], BF16)
+        staged_low = ring("staged_low", 2, [P, 2 * KL], BF16)
+        staged_y = ring("staged_y", 2, [P, 2 * N], BF16)
+        high_codes = ring("high_codes", RING, [P, HIGH * P], U32)
+        high_scales = ring("high_scales", RING, [P, HIGH * P], U8)
+        low_codes = ring("low_codes", 2, [P, 2 * P], U32)
+        low_scales = ring("low_scales", 2, [P, 2 * P], U8)
+        clamped = ring("clamped", 2, [P, 2, N], F32)
+        logs = ring("logs", 2, [P, 2, N], F32)
+        y = ring("y", PAIRS, [P, 2, N], F32)
+        y_bf = ring("y_bf", 2, [P, 2, 2, P, 2], BF16)
         y_codes = keep.tile([P, T], U32, align_bytes=64)
         y_scales = keep.tile([P, T], U8, align_bytes=64)
-        high_words = keep.tile([P, HIGH, 2 * N], U8, align_bytes=64)
-        high_scales = keep.tile([P, HIGH, N], U8, align_bytes=64)
-        low_raw = keep.tile([P, 4, N], BF16, align_bytes=64)
-        low_grouped = keep.tile([P, N, 4], BF16, align_bytes=64)
-        low_codes = keep.tile([P, N], U32, align_bytes=64)
-        low_scales = keep.tile([P, N], U8, align_bytes=64)
+        wh_words = keep.tile([P, HIGH, 2 * N], U8, align_bytes=64)
+        wh_scales = keep.tile([P, HIGH, N], U8, align_bytes=64)
+        wl_raw = keep.tile([P, 4, N], BF16, align_bytes=64)
+        wl_grouped = keep.tile([P, N, 4], BF16, align_bytes=64)
+        wl_codes = keep.tile([P, N], U32, align_bytes=64)
+        wl_scales = keep.tile([P, N], U8, align_bytes=64)
         least_col = keep.tile([P, 4], BF16, align_bytes=64)
         gain_col = keep.tile([P, 4], BF16, align_bytes=64)
         band_rows = keep.tile([P, 2, N], BF16, align_bytes=64)
@@ -69,114 +73,132 @@ def tile_split_band_log_mel_g5_kernel(
         energy = [psum.tile([P, N], F32, name=f"energy{i}") for i in range(2)]
 
         ctx.enter_context(tc.manual_schedule())
+        vector_copy, scalar_copy = nc.vector.tensor_copy, nc.scalar.copy
+        both = slice(0, 2)
 
-        def load_power(i, pieces):
-            rows = slice(i * P, (i + 1) * P)
+        def frames(ap, k, tiles):
+            rows = ap[2 * k * P : 2 * (k + 1) * P, :].rearrange("(j m) c -> m j c", j=2)
+            return rows[:, tiles, :]
+
+        def load_high(i, pieces=1):
             step = KH // pieces
             for c in range(0, KH, step):
-                nc.sync.dma_start(out=power[i][:, c : c + step], in_=power_high[rows, c : c + step])
-            nc.sync.dma_start(out=power[i][:, KH:], in_=power_low[rows, :])
-
-        def sorted_by(i, g):
-            if i < FIRST_SORTED or i >= TILES:
-                return None
-            return "v" if g in V_SORT else "s" if g in S_SORT else None
-
-        def sort(i, who):
-            gs = [g for g in range(PASSES) if sorted_by(i, g) == who]
-            if not gs:
-                return
-            lo, hi = gs[0], gs[-1] + 1
-            src = power[i][:].bitcast(F32)[:, lo * WORDS : hi * WORDS].rearrange("m (g p u) -> m g u p", u=2, p=P)
-            dst = sorted_words[i % RING][:, lo:hi, :, :]
-            if who == "v":
-                nc.vector.tensor_copy(out=dst, in_=src)
-            else:
-                nc.scalar.copy(out=dst, in_=src)
-
-        def bank_of(s, slot):
-            return turn[3 * (s % 2) + slot // 2]
-
-        def transposes(s):
-            if s < TILES:
-                words = power[s][:].bitcast(F32)
-                for g in range(PASSES):
-                    for u in range(2):
-                        if sorted_by(s, g):
-                            src = sorted_words[s % RING][:, g, u, :]
-                        else:
-                            src = words[:, g * WORDS + u : (g + 1) * WORDS : 2]
-                        nc.tensor.transpose(bank_of(s, g)[:, 2 * (g % 2) + u, :], src, ident[:])
-            j = s - Y_LAG
-            if 0 <= j < TILES:
-                pairs = y_bf[j % RING][:].rearrange("m u p e -> m (u p e)").bitcast(F32)
-                for u in range(2):
-                    nc.tensor.transpose(bank_of(s, PASSES)[:, 2 + u, :], pairs[:, u * P : (u + 1) * P], ident[:])
-
-        def copy_out(s, b, copy=nc.scalar.copy):
-            lo, hi = 2 * b, 2 * b + 2
-            if s >= TILES:
-                lo = max(lo, PASSES)
-            if not 0 <= s - Y_LAG < TILES:
-                hi = min(hi, PASSES)
-            if lo >= hi:
-                return
-            dst = staged[s % RING][:].bitcast(F32)[:, lo * WORDS : hi * WORDS].rearrange("p (g m u) -> p g m u", u=2, m=P)
-            src = bank_of(s, lo)[:, 2 * (lo % 2) : 2 * (lo % 2) + 2 * (hi - lo), :].rearrange("p (g u) m -> p g m u", u=2)
-            copy(out=dst, in_=src)
-
-        def quantize_power(s, lo, hi):
-            if 0 <= s < TILES:
-                nc.vector.quantize_mx(
-                    out=codes[s % RING][:, lo * P : hi * P].bitcast(FP8X4),
-                    scales=scales[s % RING][:, lo * P : hi * P],
-                    in_=staged[s % RING][:, lo * 512 : hi * 512],
+                nc.sync.dma_start(
+                    out=high[i // 2][:, i % 2, c : c + step], in_=power_high[i * P : (i + 1) * P, c : c + step]
                 )
 
-        def quantize_y(j):
-            if 0 <= j < TILES:
-                cols = slice(j * P, (j + 1) * P)
-                nc.vector.quantize_mx(
-                    out=y_codes[:, cols].bitcast(FP8X4),
-                    scales=y_scales[:, cols],
-                    in_=staged[(j + Y_LAG) % RING][:, PASSES * 512 :],
-                )
+        def load_low(k):
+            nc.sync.dma_start(out=low[k][:], in_=frames(power_low, k, both))
+
+        def sort(k, passes, copy):
+            if not passes or not FIRST_SORTED <= k < PAIRS:
+                return
+            lo, hi = passes[0], passes[-1] + 1
+            src = high[k][:].bitcast(F32)[:, :, lo * WORDS : hi * WORDS]
+            copy(
+                out=sorted_words[k % 3][:, :, lo:hi, :, :],
+                in_=src.rearrange("m j (g p u) -> m j g u p", u=2, p=P),
+            )
+
+        def transpose_pair(bank, slot, words):
+            for u in range(2):
+                nc.tensor.transpose(bank[:, 2 * slot + u, :], words[u], ident[:])
+
+        def every_other(words):
+            return [words[:, u : WORDS : 2] for u in range(2)]
+
+        def turn_high(i):
+            k, j = divmod(i, 2)
+            for g in range(HIGH):
+                if k >= FIRST_SORTED and g in V_SORT + S_SORT:
+                    words = [sorted_words[k % 3][:, j, g, u, :] for u in range(2)]
+                else:
+                    words = every_other(high[k][:, j, g * 512 : (g + 1) * 512].bitcast(F32))
+                transpose_pair(turn[3 * j + g // 2], g % 2, words)
+
+        def turn_low(k):
+            for j in range(2):
+                transpose_pair(turn[2], j, every_other(low[k][:, j, :].bitcast(F32)))
+
+        def turn_y(k, tiles=both, bank=5):
+            if k >= 0:
+                for j in range(2)[tiles]:
+                    words = y_bf[k % 2][:, j].rearrange("m u p e -> m u (p e)").bitcast(F32)
+                    transpose_pair(turn[bank], j, [words[:, u, :] for u in range(2)])
+
+        def copy_out(bank, dst, slots=both, copy=scalar_copy):
+            words = dst.bitcast(F32).rearrange("p (g m u) -> p g m u", u=2, m=P)
+            copy(out=words[:, slots], in_=turn[bank][:].rearrange("p (g u) m -> p g m u", u=2)[:, slots])
+
+        def copy_high(i, half, copy=scalar_copy):
+            copy_out(3 * (i % 2) + half, staged_high[i % RING][:, half * 1024 : (half + 1) * 1024], copy=copy)
+
+        def copy_low(k):
+            copy_out(2, staged_low[k % 2][:])
+
+        def copy_y(k, tiles=both, bank=5, copy=scalar_copy):
+            if k >= 0:
+                copy_out(bank, staged_y[k % 2][:], tiles, copy)
+
+        def quantize(codes, scales, values):
+            nc.vector.quantize_mx(out=codes.bitcast(FP8X4), scales=scales, in_=values)
+
+        def quantize_high(i):
+            quantize(high_codes[i % RING][:], high_scales[i % RING][:], staged_high[i % RING][:])
+
+        def quantize_low(k):
+            quantize(low_codes[k % 2][:], low_scales[k % 2][:], staged_low[k % 2][:])
 
         def matmuls(i):
-            if not 0 <= i < TILES:
-                return
-            for g in range(PASSES):
-                cols = slice(g * P, (g + 1) * P)
-                if g == LOW:
-                    rhs, rhs_scale = low_codes[:].bitcast(FP8X4), low_scales[:]
+            k, j = divmod(i, 2)
+            for g in range(HIGH + 1):
+                if g < HIGH:
+                    cols = slice(g * P, (g + 1) * P)
+                    codes, scales = high_codes[i % RING][:, cols], high_scales[i % RING][:, cols]
+                    rhs, rhs_scale = wh_words[:, g, :].bitcast(FP4X4), wh_scales[:, g, :]
                 else:
-                    rhs, rhs_scale = high_words[:, g, :].bitcast(FP4X4), high_scales[:, g, :]
+                    cols = slice(j * P, (j + 1) * P)
+                    codes, scales = low_codes[k % 2][:, cols], low_scales[k % 2][:, cols]
+                    rhs, rhs_scale = wl_codes[:].bitcast(FP8X4), wl_scales[:]
                 nc.tensor.matmul_mx(
-                    out=energy[i % 2][:], lhsT=codes[i % RING][:, cols].bitcast(FP8X4), lhsT_scale=scales[i % RING][:, cols],
-                    rhs=rhs, rhs_scale=rhs_scale, start=(g == 0), stop=(g == PASSES - 1),
+                    out=energy[j][:], lhsT=codes.bitcast(FP8X4), lhsT_scale=scales,
+                    rhs=rhs, rhs_scale=rhs_scale, start=(g == 0), stop=(g == HIGH),
                 )
 
-        def clamp(j):
-            if 0 <= j < TILES:
-                nc.vector.tensor_tensor(out=clamped[j % 2][:], in0=energy[j % 2][:], in1=band_rows[:, 0, :], op=ALU.max)
+        def clamp(i):
+            if i >= 0:
+                k, j = divmod(i, 2)
+                nc.vector.tensor_tensor(out=clamped[k % 2][:, j, :], in0=energy[j][:], in1=band_rows[:, 0, :], op=ALU.max)
 
-        def log(j):
-            if 0 <= j < TILES:
-                nc.scalar.activation(out=logs[j % RING][:], in_=clamped[j % 2][:], func=ACT.Ln)
+        def log(k, tiles=both):
+            if k >= 0:
+                nc.scalar.activation(out=logs[k % 2][:, tiles, :], in_=clamped[k % 2][:, tiles, :], func=ACT.Ln)
 
-        def scale_and_store(j):
-            if 0 <= j < TILES:
-                nc.vector.tensor_tensor(out=y[j][:], in0=logs[j % RING][:], in1=band_rows[:, 1, :], op=ALU.mult)
-                nc.sync.dma_start(out=out_0[j * P : (j + 1) * P, :], in_=y[j][:])
+        def scale_and_store(k, tiles=both):
+            if k >= 0:
+                count = len(range(2)[tiles])
+                nc.vector.tensor_tensor(
+                    out=y[k][:, tiles, :], in0=logs[k % 2][:, tiles, :],
+                    in1=band_rows[:, 1:2, :].to_broadcast([P, count, N]), op=ALU.mult,
+                )
+                nc.sync.dma_start(out=frames(out_0, k, tiles), in_=y[k][:, tiles, :])
 
-        def round_y(j, copy=nc.vector.tensor_copy):
-            if 0 <= j < TILES:
-                copy(out=y_bf[j % RING][:], in_=y[j][:].rearrange("m (p u e) -> m u p e", u=2, e=2))
+        def round_y(k, tiles=both, copy=vector_copy):
+            if k >= 0:
+                copy(
+                    out=y_bf[k % 2][:, tiles],
+                    in_=y[k][:, tiles, :].rearrange("m j (p u e) -> m j u p e", u=2, e=2),
+                )
 
         out_words = out_1[0].rearrange("p m t -> p (m t)").bitcast(I32)
         out_scales = out_2[0].bitcast(I32)
 
-        def store_planes(lo, hi):
+        def quantize_y(k, tiles=both):
+            if k >= 0:
+                cols = slice((2 * k + tiles.start) * P, (2 * k + tiles.stop) * P)
+                quantize(y_codes[:, cols], y_scales[:, cols], staged_y[k % 2][:, tiles.start * N : tiles.stop * N])
+
+        def store_words(lo, hi):
             nc.sync.dma_start(out=out_words[:, lo * P : hi * P], in_=y_codes[:, lo * P : hi * P].bitcast(I32))
 
         def store_scales(lo, hi):
@@ -186,23 +208,6 @@ def tile_split_band_log_mel_g5_kernel(
                     out=out_scales[4 * q : 4 * q + 4, lo * P // 4 : hi * P // 4],
                     in_=y_scales[32 * q : 32 * q + 4, lo * P : hi * P].bitcast(I32),
                 )
-
-        nc.vector.memset(high_scales[:].rearrange("p g n -> p (g n)").bitcast(I32), 0)
-        nc.vector.memset(warm[:, 0:1], 1.0)
-        nc.scalar.activation(out=warm[:, 1:2], in_=warm[:, 0:1], func=ACT.Ln)
-        make_identity(nc, ident[:])
-        load_power(0, 2)
-        nc.sync.dma_start(out=least_col[:], in_=least_energy.rearrange("(p t) -> p t", t=4))
-        nc.sync.dma_start(out=gain_col[:], in_=gain.rearrange("(p t) -> p t", t=4))
-        nc.sync.dma_start(out=low_raw[:], in_=bank_low.rearrange("(p t) n -> p t n", t=4))
-        for q in range(4):
-            nc.sync.dma_start(
-                out=high_scales[32 * q : 32 * q + 4, :, :].bitcast(I32),
-                in_=bank_high_scales[:, 4 * q : 4 * q + 4, :].bitcast(I32).rearrange("g r n -> r g n"),
-            )
-        nc.sync.dma_start(out=high_words[:].bitcast(I32), in_=bank_high_words.bitcast(I32).rearrange("g p w -> p g w"))
-        for i in range(1, TILES):
-            load_power(i, 1)
 
         band_bank = energy[1][:].rearrange("p (v m) -> p v m", m=P)
 
@@ -220,84 +225,128 @@ def tile_split_band_log_mel_g5_kernel(
 
         def group_bank_low(copy, cols):
             copy(
-                out=low_grouped[:, cols, :].rearrange("p (c i) t -> p c t i", i=4),
-                in_=low_raw[:, :, cols].rearrange("p t (c i) -> p c t i", i=4),
+                out=wl_grouped[:, cols, :].rearrange("p (c i) t -> p c t i", i=4),
+                in_=wl_raw[:, :, cols].rearrange("p t (c i) -> p c t i", i=4),
             )
 
-        def quantize_bank_low():
-            nc.vector.quantize_mx(
-                out=low_codes[:].bitcast(FP8X4), scales=low_scales[:], in_=low_grouped[:].rearrange("p n t -> p (n t)")
+        nc.vector.memset(wh_scales[:].rearrange("p g n -> p (g n)").bitcast(I32), 0)
+        nc.vector.memset(warm[:, 0:1], 1.0)
+        nc.scalar.activation(out=warm[:, 1:2], in_=warm[:, 0:1], func=ACT.Ln)
+        make_identity(nc, ident[:])
+        load_high(0, 2)
+        load_low(0)
+        nc.sync.dma_start(out=least_col[:], in_=least_energy.rearrange("(p t) -> p t", t=4))
+        nc.sync.dma_start(out=gain_col[:], in_=gain.rearrange("(p t) -> p t", t=4))
+        nc.sync.dma_start(out=wl_raw[:], in_=bank_low.rearrange("(p t) n -> p t n", t=4))
+        for q in range(4):
+            nc.sync.dma_start(
+                out=wh_scales[32 * q : 32 * q + 4, :, :].bitcast(I32),
+                in_=bank_high_scales[:, 4 * q : 4 * q + 4, :].bitcast(I32).rearrange("g r n -> r g n"),
             )
+        nc.sync.dma_start(out=wh_words[:].bitcast(I32), in_=bank_high_words.bitcast(I32).rearrange("g p w -> p g w"))
+        load_high(1)
+        for k in range(1, PAIRS):
+            load_high(2 * k)
+            load_low(k)
+            load_high(2 * k + 1)
 
-        def planes(j):
-            quantize_y(j)
-            done = j + 1
-            if done in (4, 8, 12, 15, 16):
-                store_planes({4: 0, 8: 4, 12: 8, 15: 12, 16: 15}[done], done)
-            if done in (12, 16):
-                store_scales(done - 12 if done == 12 else 12, done)
-
-        vector_copy = nc.vector.tensor_copy
-
-        transposes(0)
+        first, second = slice(0, 1), slice(1, 2)
+        turn_high(0)
+        turn_low(0)
         spread_band_vectors()
-        copy_out(0, 0)
-        copy_out(0, 1, vector_copy)
-        group_bank_low(nc.scalar.copy, slice(LOW_V, N))
+        copy_high(0, 0)
+        copy_high(0, 1, vector_copy)
+        group_bank_low(scalar_copy, slice(LOW_V, N))
         group_bank_low(vector_copy, slice(0, LOW_V))
-        copy_out(0, 2)
-        quantize_power(0, 0, HIGH)
-        quantize_bank_low()
-        quantize_power(0, LOW, PASSES)
+        copy_low(0)
+        quantize_high(0)
+        quantize(wl_codes[:], wl_scales[:], wl_grouped[:].rearrange("p n t -> p (n t)"))
+        quantize_low(0)
         copy_band_vectors()
         matmuls(0)
 
-        transposes(1)
+        turn_high(1)
         clamp(0)
-        copy_out(1, 0)
-        sort(2, "v")
-        sort(2, "s")
-        copy_out(1, 1, vector_copy)
-        copy_out(1, 2)
-        log(0)
-        quantize_power(1, 0, HIGH)
-        quantize_power(1, LOW, PASSES)
-        sort(3, "s")
-        sort(3, "v")
+        copy_high(1, 0)
+        copy_high(1, 1, vector_copy)
+        quantize_high(1)
 
-        for s in range(2, TILES):
-            transposes(s)
-            for b in range(3):
-                copy_out(s, b)
-            matmuls(s - 1)
-            sort(s + 2, "v")
-            quantize_power(s, 0, HIGH)
-            quantize_power(s, LOW, PASSES)
-            if s > 2:
-                log(s - 2)
-            clamp(s - 1)
-            scale_and_store(s - 2)
-            sort(s + 2, "s")
-            planes(s - Y_LAG)
-            round_y(s - 2)
+        for k in range(1, PAIRS - 1):
+            i = 2 * k
+            turn_high(i)
+            turn_low(k)
+            if k > 1:
+                clamp(i - 2)
+            scale_and_store(k - 2)
+            copy_high(i, 0)
+            copy_high(i, 1)
+            copy_low(k)
+            matmuls(i - 1)
+            quantize_high(i)
+            round_y(k - 2)
+            sort(k + 1, S_SORT, scalar_copy)
 
+            turn_high(i + 1)
+            turn_y(k - 2)
+            clamp(i - 1)
+            quantize_low(k)
+            sort(k + 1, V_SORT, vector_copy)
+            copy_high(i + 1, 0)
+            copy_high(i + 1, 1)
+            copy_y(k - 2)
+            matmuls(i)
+            quantize_high(i + 1)
+            log(k - 1)
+            quantize_y(k - 2)
+            if k in (3, 5):
+                store_words(2 * k - 6, 2 * k - 2)
+
+        turn_high(14)
+        turn_low(7)
+        turn_high(15)
+        clamp(12)
+        scale_and_store(5)
+        matmuls(13)
+        copy_high(14, 0)
+        copy_high(14, 1)
+        copy_low(7)
+        log(6, first)
+        copy_high(15, 0)
+        quantize_high(14)
+        round_y(5)
+        quantize_low(7)
+        copy_high(15, 1)
+        turn_y(5)
+        matmuls(14)
+        copy_y(5)
+        clamp(13)
+        quantize_high(15)
+        scale_and_store(6, first)
+        quantize_y(5)
         matmuls(15)
-        transposes(16)
-        log(14)
-        copy_out(16, 2)
-        transposes(17)
+        log(6, second)
+        store_words(8, 12)
+        scale_and_store(6, second)
+        round_y(6, second, scalar_copy)
+        clamp(14)
         clamp(15)
-        scale_and_store(14)
-        log(15)
-        copy_out(17, 2)
-        planes(12)
-        round_y(14)
-        scale_and_store(15)
-        transposes(18)
-        planes(13)
-        round_y(15)
-        copy_out(18, 2)
-        transposes(19)
-        copy_out(19, 2)
-        planes(14)
-        planes(15)
+        store_scales(0, 12)
+        round_y(6, first)
+        log(7, first)
+        turn_y(6)
+        scale_and_store(7, first)
+        log(7, second)
+        round_y(7, first, scalar_copy)
+        scale_and_store(7, second)
+        copy_y(6)
+        turn_y(7, first, 2)
+        round_y(7, second)
+        copy_y(7, first, 2)
+        turn_y(7, second, 4)
+        quantize_y(6)
+        store_words(12, 14)
+        copy_y(7, second, 4)
+        quantize_y(7, first)
+        quantize_y(7, second)
+        store_words(14, 16)
+        store_scales(12, 16)

@@ -246,8 +246,8 @@ def tile_split_band_log_mel_g5_kernel(
         nc.sync.dma_start(out=wh_words[:].bitcast(I32), in_=bank_high_words.bitcast(I32).rearrange("g p w -> p g w"))
         load_high(1)
         for k in range(1, PAIRS):
-            load_high(2 * k)
             load_low(k)
+            load_high(2 * k)
             load_high(2 * k + 1)
 
         first, second = slice(0, 1), slice(1, 2)
@@ -273,43 +273,45 @@ def tile_split_band_log_mel_g5_kernel(
 
         for k in range(1, PAIRS - 1):
             i = 2 * k
-            turn_high(i)
+            turn_y(k - 3)
             turn_low(k)
+            turn_high(i)
+            turn_high(i + 1)
             if k > 1:
                 clamp(i - 2)
+            copy_y(k - 3)
             scale_and_store(k - 2)
             copy_high(i, 0)
             copy_high(i, 1)
             copy_low(k)
             matmuls(i - 1)
+            quantize_y(k - 3)
             quantize_high(i)
             round_y(k - 2)
-            sort(k + 1, S_SORT, scalar_copy)
-
-            turn_high(i + 1)
-            turn_y(k - 2)
-            clamp(i - 1)
             quantize_low(k)
-            sort(k + 1, V_SORT, vector_copy)
+            matmuls(i)
             copy_high(i + 1, 0)
             copy_high(i + 1, 1)
-            copy_y(k - 2)
-            matmuls(i)
+            clamp(i - 1)
+            sort(k + 1, S_SORT, scalar_copy)
+            sort(k + 1, V_SORT, vector_copy)
             quantize_high(i + 1)
             log(k - 1)
-            quantize_y(k - 2)
-            if k in (3, 5):
-                store_words(2 * k - 6, 2 * k - 2)
+            if k in (4, 6):
+                store_words(2 * k - 8, 2 * k - 4)
 
-        turn_high(14)
+        turn_y(4)
         turn_low(7)
+        turn_high(14)
         turn_high(15)
         clamp(12)
+        copy_y(4)
         scale_and_store(5)
         matmuls(13)
         copy_high(14, 0)
         copy_high(14, 1)
         copy_low(7)
+        quantize_y(4)
         log(6, first)
         copy_high(15, 0)
         quantize_high(14)

@@ -22,9 +22,10 @@ PAIRS = TILES // 2
 HIGH = KH // 512
 WORDS = 256
 
-V_SORT = (0, 1)
-S_SORT = (2,)
-FIRST_SORTED = 2
+SORTED0 = 2
+SORTED1 = 3
+WORD_LOADS = 2
+FIRST_SORTED = 4
 LOW_V = 352
 RING = 4
 LONG_RUNS = 0
@@ -90,15 +91,13 @@ def tile_split_band_log_mel_g5_kernel(
         def load_low(k):
             nc.sync.dma_start(out=low[k][:], in_=frames(power_low, k, both))
 
-        def sort(k, passes, copy):
-            if not passes or not FIRST_SORTED <= k < PAIRS:
+        def sort(i, copy):
+            k, j = divmod(i, 2)
+            count = (SORTED0, SORTED1)[j]
+            if not count or not FIRST_SORTED <= i < TILES:
                 return
-            lo, hi = passes[0], passes[-1] + 1
-            src = high[k][:].bitcast(F32)[:, :, lo * WORDS : hi * WORDS]
-            copy(
-                out=sorted_words[k % 3][:, :, lo:hi, :, :],
-                in_=src.rearrange("m j (g p u) -> m j g u p", u=2, p=P),
-            )
+            src = high[k][:, j, : count * 512].bitcast(F32)
+            copy(out=sorted_words[k % 3][:, j, :count, :, :], in_=src.rearrange("m (g p u) -> m g u p", u=2, p=P))
 
         def transpose_pair(bank, slot, words):
             for u in range(2):
@@ -110,7 +109,7 @@ def tile_split_band_log_mel_g5_kernel(
         def turn_high(i):
             k, j = divmod(i, 2)
             for g in range(HIGH):
-                if k >= FIRST_SORTED and g in V_SORT + S_SORT:
+                if i >= FIRST_SORTED and g < (SORTED0, SORTED1)[j]:
                     words = [sorted_words[k % 3][:, j, g, u, :] for u in range(2)]
                 else:
                     words = every_other(high[k][:, j, g * 512 : (g + 1) * 512].bitcast(F32))
@@ -190,6 +189,49 @@ def tile_split_band_log_mel_g5_kernel(
                     in_=y[k][:, tiles, :].rearrange("m j (p u e) -> m j u p e", u=2, e=2),
                 )
 
+        def half_bank(h):
+            return (turn[0][:].rearrange("p g m -> p (g m)"), energy[1][:])[h][:, : N // 2]
+
+        def half_matmuls(h):
+            i = TILES - 1
+            for q in range(2):
+                bands = slice((2 * h + q) * P, (2 * h + q + 1) * P)
+                for g in range(HIGH + 1):
+                    if g < HIGH:
+                        cols = slice(g * P, (g + 1) * P)
+                        codes, scales = high_codes[i % RING][:, cols], high_scales[i % RING][:, cols]
+                        rhs = wh_words[:, g, 2 * bands.start : 2 * bands.stop].bitcast(FP4X4)
+                        rhs_scale = wh_scales[:, g, bands]
+                    else:
+                        codes, scales = low_codes[1][:, P:], low_scales[1][:, P:]
+                        rhs, rhs_scale = wl_codes[:, bands].bitcast(FP8X4), wl_scales[:, bands]
+                    nc.tensor.matmul_mx(
+                        out=half_bank(h)[:, q * P : (q + 1) * P], lhsT=codes.bitcast(FP8X4), lhsT_scale=scales,
+                        rhs=rhs, rhs_scale=rhs_scale, start=(g == 0), stop=(g == HIGH),
+                    )
+
+        def half(h):
+            return slice(h * N // 2, (h + 1) * N // 2)
+
+        def half_clamp(h):
+            nc.vector.tensor_tensor(out=clamped[1][:, 1, half(h)], in0=half_bank(h), in1=band_rows[:, 0, half(h)], op=ALU.max)
+
+        def half_log(h):
+            nc.scalar.activation(out=logs[1][:, 1, half(h)], in_=clamped[1][:, 1, half(h)], func=ACT.Ln)
+
+        def half_scale(h):
+            nc.vector.tensor_tensor(
+                out=y[7][:, 1, half(h)], in0=logs[1][:, 1, half(h)], in1=band_rows[:, 1, half(h)], op=ALU.mult
+            )
+            if h:
+                nc.sync.dma_start(out=frames(out_0, 7, slice(1, 2)), in_=y[7][:, 1:2, :])
+
+        def half_round(h, copy=vector_copy):
+            copy(
+                out=y_bf[1][:, 1, :, h * 64 : (h + 1) * 64, :],
+                in_=y[7][:, 1, half(h)].rearrange("m (p u e) -> m u p e", u=2, e=2),
+            )
+
         out_words = out_1[0].rearrange("p m t -> p (m t)").bitcast(I32)
         out_scales = out_2[0].bitcast(I32)
 
@@ -234,16 +276,20 @@ def tile_split_band_log_mel_g5_kernel(
         nc.scalar.activation(out=warm[:, 1:2], in_=warm[:, 0:1], func=ACT.Ln)
         make_identity(nc, ident[:])
         load_high(0, 2)
-        load_low(0)
         nc.sync.dma_start(out=least_col[:], in_=least_energy.rearrange("(p t) -> p t", t=4))
         nc.sync.dma_start(out=gain_col[:], in_=gain.rearrange("(p t) -> p t", t=4))
         nc.sync.dma_start(out=wl_raw[:], in_=bank_low.rearrange("(p t) n -> p t n", t=4))
+        load_low(0)
         for q in range(4):
             nc.sync.dma_start(
                 out=wh_scales[32 * q : 32 * q + 4, :, :].bitcast(I32),
                 in_=bank_high_scales[:, 4 * q : 4 * q + 4, :].bitcast(I32).rearrange("g r n -> r g n"),
             )
-        nc.sync.dma_start(out=wh_words[:].bitcast(I32), in_=bank_high_words.bitcast(I32).rearrange("g p w -> p g w"))
+        for g in range(0, HIGH, HIGH // WORD_LOADS):
+            gs = slice(g, g + HIGH // WORD_LOADS)
+            nc.sync.dma_start(
+                out=wh_words[:, gs, :].bitcast(I32), in_=bank_high_words[gs].bitcast(I32).rearrange("g p w -> p g w")
+            )
         load_high(1)
         for k in range(1, PAIRS):
             load_low(k)
@@ -252,14 +298,14 @@ def tile_split_band_log_mel_g5_kernel(
 
         first, second = slice(0, 1), slice(1, 2)
         turn_high(0)
-        turn_low(0)
         spread_band_vectors()
-        copy_high(0, 0)
-        copy_high(0, 1, vector_copy)
-        group_bank_low(scalar_copy, slice(LOW_V, N))
+        turn_low(0)
         group_bank_low(vector_copy, slice(0, LOW_V))
-        copy_low(0)
+        copy_high(0, 0)
+        copy_high(0, 1)
         quantize_high(0)
+        group_bank_low(scalar_copy, slice(LOW_V, N))
+        copy_low(0)
         quantize(wl_codes[:], wl_scales[:], wl_grouped[:].rearrange("p n t -> p (n t)"))
         quantize_low(0)
         copy_band_vectors()
@@ -293,8 +339,8 @@ def tile_split_band_log_mel_g5_kernel(
             copy_high(i + 1, 0)
             copy_high(i + 1, 1)
             clamp(i - 1)
-            sort(k + 1, S_SORT, scalar_copy)
-            sort(k + 1, V_SORT, vector_copy)
+            sort(i + 3, scalar_copy)
+            sort(i + 2, vector_copy)
             quantize_high(i + 1)
             log(k - 1)
             if k in (4, 6):
@@ -312,41 +358,41 @@ def tile_split_band_log_mel_g5_kernel(
         copy_high(14, 1)
         copy_low(7)
         quantize_y(4)
-        log(6, first)
-        copy_high(15, 0)
-        quantize_high(14)
         round_y(5)
+        quantize_high(14)
         quantize_low(7)
-        copy_high(15, 1)
         turn_y(5)
         matmuls(14)
-        copy_y(5)
+        copy_high(15, 0)
+        copy_high(15, 1)
         clamp(13)
         quantize_high(15)
-        scale_and_store(6, first)
-        quantize_y(5)
         matmuls(15)
+        log(6, first)
         log(6, second)
-        store_words(8, 12)
+        copy_y(5)
+        scale_and_store(6, first)
         scale_and_store(6, second)
-        round_y(6, second, scalar_copy)
         clamp(14)
-        clamp(15)
+        quantize_y(5)
+        store_words(8, 12)
         store_scales(0, 12)
+        clamp(15)
+        round_y(6, second, scalar_copy)
         round_y(6, first)
         log(7, first)
+        log(7, second)
         turn_y(6)
         scale_and_store(7, first)
-        log(7, second)
-        round_y(7, first, scalar_copy)
         scale_and_store(7, second)
+        round_y(7, first, scalar_copy)
+        round_y(7, second)
         copy_y(6)
         turn_y(7, first, 2)
-        round_y(7, second)
-        copy_y(7, first, 2)
         turn_y(7, second, 4)
         quantize_y(6)
         store_words(12, 14)
+        copy_y(7, first, 2)
         copy_y(7, second, 4)
         quantize_y(7, first)
         quantize_y(7, second)

from contextlib import ExitStack

import concourse.mybir as mybir
from concourse.masks import make_identity

T, KL, KH, N = 2048, 512, 2048, 512
FLOPS = 2 * T * (KL + KH) * N

F32 = mybir.dt.float32
BF16 = mybir.dt.bfloat16
I32 = mybir.dt.int32
U32 = mybir.dt.uint32
U8 = mybir.dt.uint8
FP8X4 = mybir.dt.float8_e4m3fn_x4
FP4X4 = mybir.dt.float4_e2m1fn_x4
ALU = mybir.AluOpType
ACT = mybir.ActivationFunctionType

P = 128
TILES = T // P
PAIRS = TILES // 2
HIGH = KH // 512
WORDS = 256

SORTED0 = 2
SORTED1 = 3
WORD_LOADS = 2
FIRST_SORTED = 4
LOW_V = 352
RING = 4
LONG_RUNS = 0


def tile_split_band_log_mel_g5_kernel(
    tc, power_low, power_high, bank_low, bank_high_words, bank_high_scales, least_energy, gain,
    out_0, out_1, out_2,
):
    nc = tc.nc
    with ExitStack() as ctx:
        keep = ctx.enter_context(tc.tile_pool(name="keep", bufs=1))
        psum = ctx.enter_context(tc.psum_pool(name="psum", bufs=1))

        def ring(label, count, shape, dtype):
            return [keep.tile(shape, dtype, name=f"{label}{i}", align_bytes=64) for i in range(count)]

        high = ring("high", PAIRS, [P, 2, KH], BF16)
        low = ring("low", PAIRS, [P, 2, KL], BF16)
        sorted_words = ring("sorted", 3, [P, 2, HIGH, 2, P], F32)
        staged_high = ring("staged_high", RING, [P, KH], BF16)
        staged_low = ring("staged_low", 2, [P, 2 * KL], BF16)
        staged_y = ring("staged_y", 2, [P, 2 * N], BF16)
        high_codes = ring("high_codes", RING, [P, HIGH * P], U32)
        high_scales = ring("high_scales", RING, [P, HIGH * P], U8)
        low_codes = ring("low_codes", 2, [P, 2 * P], U32)
        low_scales = ring("low_scales", 2, [P, 2 * P], U8)
        clamped = ring("clamped", 2, [P, 2, N], F32)
        logs = ring("logs", 2, [P, 2, N], F32)
        y = ring("y", PAIRS, [P, 2, N], F32)
        y_bf = ring("y_bf", 2, [P, 2, 2, P, 2], BF16)
        y_codes = keep.tile([P, T], U32, align_bytes=64)
        y_scales = keep.tile([P, T], U8, align_bytes=64)
        wh_words = keep.tile([P, HIGH, 2 * N], U8, align_bytes=64)
        wh_scales = keep.tile([P, HIGH, N], U8, align_bytes=64)
        wl_raw = keep.tile([P, 4, N], BF16, align_bytes=64)
        wl_grouped = keep.tile([P, N, 4], BF16, align_bytes=64)
        wl_codes = keep.tile([P, N], U32, align_bytes=64)
        wl_scales = keep.tile([P, N], U8, align_bytes=64)
        least_col = keep.tile([P, 4], BF16, align_bytes=64)
        gain_col = keep.tile([P, 4], BF16, align_bytes=64)
        band_rows = keep.tile([P, 2, N], BF16, align_bytes=64)
        ident = keep.tile([P, P], F32, align_bytes=64)
        warm = keep.tile([P, 2], F32, align_bytes=64)
        turn = [psum.tile([P, 4, P], F32, name=f"turn{i}") for i in range(6)]
        energy = [psum.tile([P, N], F32, name=f"energy{i}") for i in range(2)]

        ctx.enter_context(tc.manual_schedule())
        vector_copy, scalar_copy = nc.vector.tensor_copy, nc.scalar.copy
        both = slice(0, 2)

        def frames(ap, k, tiles):
            rows = ap[2 * k * P : 2 * (k + 1) * P, :].rearrange("(j m) c -> m j c", j=2)
            return rows[:, tiles, :]

        def load_high(i, pieces=1):
            step = KH // pieces
            for c in range(0, KH, step):
                nc.sync.dma_start(
                    out=high[i // 2][:, i % 2, c : c + step], in_=power_high[i * P : (i + 1) * P, c : c + step]
                )

        def load_low(k):
            nc.sync.dma_start(out=low[k][:], in_=frames(power_low, k, both))

        def sort(i, copy):
            k, j = divmod(i, 2)
            count = (SORTED0, SORTED1)[j]
            if not count or not FIRST_SORTED <= i < TILES:
                return
            src = high[k][:, j, : count * 512].bitcast(F32)
            copy(out=sorted_words[k % 3][:, j, :count, :, :], in_=src.rearrange("m (g p u) -> m g u p", u=2, p=P))

        def transpose_pair(bank, slot, words):
            for u in range(2):
                nc.tensor.transpose(bank[:, 2 * slot + u, :], words[u], ident[:])

        def every_other(words):
            return [words[:, u : WORDS : 2] for u in range(2)]

        def turn_high(i):
            k, j = divmod(i, 2)
            for g in range(HIGH):
                if i >= FIRST_SORTED and g < (SORTED0, SORTED1)[j]:
                    words = [sorted_words[k % 3][:, j, g, u, :] for u in range(2)]
                else:
                    words = every_other(high[k][:, j, g * 512 : (g + 1) * 512].bitcast(F32))
                transpose_pair(turn[3 * j + g // 2], g % 2, words)

        def turn_low(k):
            for j in range(2):
                transpose_pair(turn[2], j, every_other(low[k][:, j, :].bitcast(F32)))

        def turn_y(k, tiles=both, bank=5):
            if k >= 0:
                for j in range(2)[tiles]:
                    words = y_bf[k % 2][:, j].rearrange("m u p e -> m u (p e)").bitcast(F32)
                    transpose_pair(turn[bank], j, [words[:, u, :] for u in range(2)])

        def copy_out(bank, dst, slots=both, copy=scalar_copy):
            words = dst.bitcast(F32).rearrange("p (g m u) -> p g m u", u=2, m=P)
            copy(out=words[:, slots], in_=turn[bank][:].rearrange("p (g u) m -> p g m u", u=2)[:, slots])

        def copy_high(i, half, copy=scalar_copy):
            copy_out(3 * (i % 2) + half, staged_high[i % RING][:, half * 1024 : (half + 1) * 1024], copy=copy)

        def copy_low(k):
            copy_out(2, staged_low[k % 2][:])

        def copy_y(k, tiles=both, bank=5, copy=scalar_copy):
            if k >= 0:
                copy_out(bank, staged_y[k % 2][:], tiles, copy)

        def quantize(codes, scales, values):
            nc.vector.quantize_mx(out=codes.bitcast(FP8X4), scales=scales, in_=values)

        def quantize_high(i):
            quantize(high_codes[i % RING][:], high_scales[i % RING][:], staged_high[i % RING][:])

        def quantize_low(k):
            quantize(low_codes[k % 2][:], low_scales[k % 2][:], staged_low[k % 2][:])

        def matmuls(i):
            k, j = divmod(i, 2)
            for g in range(HIGH + 1):
                if g < HIGH:
                    cols = slice(g * P, (g + 1) * P)
                    codes, scales = high_codes[i % RING][:, cols], high_scales[i % RING][:, cols]
                    rhs, rhs_scale = wh_words[:, g, :].bitcast(FP4X4), wh_scales[:, g, :]
                else:
                    cols = slice(j * P, (j + 1) * P)
                    codes, scales = low_codes[k % 2][:, cols], low_scales[k % 2][:, cols]
                    rhs, rhs_scale = wl_codes[:].bitcast(FP8X4), wl_scales[:]
                nc.tensor.matmul_mx(
                    out=energy[j][:], lhsT=codes.bitcast(FP8X4), lhsT_scale=scales,
                    rhs=rhs, rhs_scale=rhs_scale, start=(g == 0), stop=(g == HIGH),
                )

        def clamp(i):
            if i >= 0:
                k, j = divmod(i, 2)
                nc.vector.tensor_tensor(out=clamped[k % 2][:, j, :], in0=energy[j][:], in1=band_rows[:, 0, :], op=ALU.max)

        def log(k, tiles=both):
            if k >= 0:
                nc.scalar.activation(out=logs[k % 2][:, tiles, :], in_=clamped[k % 2][:, tiles, :], func=ACT.Ln)

        def scale_and_store(k, tiles=both):
            if k >= 0:
                count = len(range(2)[tiles])
                nc.vector.tensor_tensor(
                    out=y[k][:, tiles, :], in0=logs[k % 2][:, tiles, :],
                    in1=band_rows[:, 1:2, :].to_broadcast([P, count, N]), op=ALU.mult,
                )
                nc.sync.dma_start(out=frames(out_0, k, tiles), in_=y[k][:, tiles, :])

        def round_y(k, tiles=both, copy=vector_copy):
            if k >= 0:
                copy(
                    out=y_bf[k % 2][:, tiles],
                    in_=y[k][:, tiles, :].rearrange("m j (p u e) -> m j u p e", u=2, e=2),
                )

        def half_bank(h):
            return (turn[0][:].rearrange("p g m -> p (g m)"), energy[1][:])[h][:, : N // 2]

        def half_matmuls(h):
            i = TILES - 1
            for q in range(2):
                bands = slice((2 * h + q) * P, (2 * h + q + 1) * P)
                for g in range(HIGH + 1):
                    if g < HIGH:
                        cols = slice(g * P, (g + 1) * P)
                        codes, scales = high_codes[i % RING][:, cols], high_scales[i % RING][:, cols]
                        rhs = wh_words[:, g, 2 * bands.start : 2 * bands.stop].bitcast(FP4X4)
                        rhs_scale = wh_scales[:, g, bands]
                    else:
                        codes, scales = low_codes[1][:, P:], low_scales[1][:, P:]
                        rhs, rhs_scale = wl_codes[:, bands].bitcast(FP8X4), wl_scales[:, bands]
                    nc.tensor.matmul_mx(
                        out=half_bank(h)[:, q * P : (q + 1) * P], lhsT=codes.bitcast(FP8X4), lhsT_scale=scales,
                        rhs=rhs, rhs_scale=rhs_scale, start=(g == 0), stop=(g == HIGH),
                    )

        def half(h):
            return slice(h * N // 2, (h + 1) * N // 2)

        def half_clamp(h):
            nc.vector.tensor_tensor(out=clamped[1][:, 1, half(h)], in0=half_bank(h), in1=band_rows[:, 0, half(h)], op=ALU.max)

        def half_log(h):
            nc.scalar.activation(out=logs[1][:, 1, half(h)], in_=clamped[1][:, 1, half(h)], func=ACT.Ln)

        def half_scale(h):
            nc.vector.tensor_tensor(
                out=y[7][:, 1, half(h)], in0=logs[1][:, 1, half(h)], in1=band_rows[:, 1, half(h)], op=ALU.mult
            )
            if h:
                nc.sync.dma_start(out=frames(out_0, 7, slice(1, 2)), in_=y[7][:, 1:2, :])

        def half_round(h, copy=vector_copy):
            copy(
                out=y_bf[1][:, 1, :, h * 64 : (h + 1) * 64, :],
                in_=y[7][:, 1, half(h)].rearrange("m (p u e) -> m u p e", u=2, e=2),
            )

        out_words = out_1[0].rearrange("p m t -> p (m t)").bitcast(I32)
        out_scales = out_2[0].bitcast(I32)

        def quantize_y(k, tiles=both):
            if k >= 0:
                cols = slice((2 * k + tiles.start) * P, (2 * k + tiles.stop) * P)
                quantize(y_codes[:, cols], y_scales[:, cols], staged_y[k % 2][:, tiles.start * N : tiles.stop * N])

        def store_words(lo, hi):
            nc.sync.dma_start(out=out_words[:, lo * P : hi * P], in_=y_codes[:, lo * P : hi * P].bitcast(I32))

        def store_scales(lo, hi):
            for q in range(4):
                queue = nc.scalar if (hi == TILES and q % 2) else nc.sync
                queue.dma_start(
                    out=out_scales[4 * q : 4 * q + 4, lo * P // 4 : hi * P // 4],
                    in_=y_scales[32 * q : 32 * q + 4, lo * P : hi * P].bitcast(I32),
                )

        band_bank = energy[1][:].rearrange("p (v m) -> p v m", m=P)

        def spread_band_vectors():
            for v, col in enumerate((least_col, gain_col)):
                for u in range(2):
                    src = col[:].bitcast(F32)[:, u : u + 1].to_broadcast([P, P])
                    nc.tensor.transpose(band_bank[:, 2 * v + u, :], src, ident[:])

        def copy_band_vectors():
            nc.scalar.copy(
                out=band_rows[:].rearrange("p v n -> p (v n)").bitcast(F32).rearrange("p (v m u) -> p v m u", u=2, m=P),
                in_=band_bank.rearrange("p (v u) m -> p v m u", u=2),
            )

        def group_bank_low(copy, cols):
            copy(
                out=wl_grouped[:, cols, :].rearrange("p (c i) t -> p c t i", i=4),
                in_=wl_raw[:, :, cols].rearrange("p t (c i) -> p c t i", i=4),
            )

        nc.vector.memset(wh_scales[:].rearrange("p g n -> p (g n)").bitcast(I32), 0)
        nc.vector.memset(warm[:, 0:1], 1.0)
        nc.scalar.activation(out=warm[:, 1:2], in_=warm[:, 0:1], func=ACT.Ln)
        make_identity(nc, ident[:])
        load_high(0, 2)
        nc.sync.dma_start(out=least_col[:], in_=least_energy.rearrange("(p t) -> p t", t=4))
        nc.sync.dma_start(out=gain_col[:], in_=gain.rearrange("(p t) -> p t", t=4))
        nc.sync.dma_start(out=wl_raw[:], in_=bank_low.rearrange("(p t) n -> p t n", t=4))
        load_low(0)
        for q in range(4):
            nc.sync.dma_start(
                out=wh_scales[32 * q : 32 * q + 4, :, :].bitcast(I32),
                in_=bank_high_scales[:, 4 * q : 4 * q + 4, :].bitcast(I32).rearrange("g r n -> r g n"),
            )
        for g in range(0, HIGH, HIGH // WORD_LOADS):
            gs = slice(g, g + HIGH // WORD_LOADS)
            nc.sync.dma_start(
                out=wh_words[:, gs, :].bitcast(I32), in_=bank_high_words[gs].bitcast(I32).rearrange("g p w -> p g w")
            )
        load_high(1)
        for k in range(1, PAIRS):
            load_low(k)
            load_high(2 * k)
            load_high(2 * k + 1)

        first, second = slice(0, 1), slice(1, 2)
        turn_high(0)
        spread_band_vectors()
        turn_low(0)
        group_bank_low(vector_copy, slice(0, LOW_V))
        copy_high(0, 0)
        copy_high(0, 1)
        quantize_high(0)
        group_bank_low(scalar_copy, slice(LOW_V, N))
        copy_low(0)
        quantize(wl_codes[:], wl_scales[:], wl_grouped[:].rearrange("p n t -> p (n t)"))
        quantize_low(0)
        copy_band_vectors()
        matmuls(0)

        turn_high(1)
        clamp(0)
        copy_high(1, 0)
        copy_high(1, 1, vector_copy)
        quantize_high(1)

        for k in range(1, PAIRS - 1):
            i = 2 * k
            turn_y(k - 3)
            turn_low(k)
            turn_high(i)
            turn_high(i + 1)
            if k > 1:
                clamp(i - 2)
            copy_y(k - 3)
            scale_and_store(k - 2)
            copy_high(i, 0)
            copy_high(i, 1)
            copy_low(k)
            matmuls(i - 1)
            quantize_y(k - 3)
            quantize_high(i)
            round_y(k - 2)
            quantize_low(k)
            matmuls(i)
            copy_high(i + 1, 0)
            copy_high(i + 1, 1)
            clamp(i - 1)
            sort(i + 3, scalar_copy)
            sort(i + 2, vector_copy)
            quantize_high(i + 1)
            log(k - 1)
            if k in (4, 6):
                store_words(2 * k - 8, 2 * k - 4)

        turn_y(4)
        turn_low(7)
        turn_high(14)
        turn_high(15)
        clamp(12)
        copy_y(4)
        scale_and_store(5)
        matmuls(13)
        copy_high(14, 0)
        copy_high(14, 1)
        copy_low(7)
        quantize_y(4)
        round_y(5)
        quantize_high(14)
        quantize_low(7)
        turn_y(5)
        matmuls(14)
        copy_high(15, 0)
        copy_high(15, 1)
        clamp(13)
        quantize_high(15)
        matmuls(15)
        log(6, first)
        log(6, second)
        copy_y(5)
        scale_and_store(6, first)
        scale_and_store(6, second)
        clamp(14)
        quantize_y(5)
        store_words(8, 12)
        store_scales(0, 12)
        clamp(15)
        round_y(6, second, scalar_copy)
        round_y(6, first)
        log(7, first)
        log(7, second)
        turn_y(6)
        scale_and_store(7, first)
        scale_and_store(7, second)
        round_y(7, first, scalar_copy)
        round_y(7, second)
        copy_y(6)
        turn_y(7, first, 2)
        turn_y(7, second, 4)
        quantize_y(6)
        store_words(12, 14)
        copy_y(7, first, 2)
        copy_y(7, second, 4)
        quantize_y(7, first)
        quantize_y(7, second)
        store_words(14, 16)
        store_scales(12, 16)
